import numpy as np, ml_dtypes
CORES = [25,29,65,69,153,157,193,197]
N = 8
import mx_ref
BF = ml_dtypes.bfloat16
def entries(a):
    return np.ascontiguousarray(a.T).reshape(-1)
def table(e):
    return np.ascontiguousarray(np.reshape(e, (-1, 16)).T).astype(np.int32)
def gcols(t, e):
    v = np.concatenate([t.reshape(8, 16, -1, 4), np.zeros((8, 16, 1, 4), BF)], axis=2)
    return np.ascontiguousarray(np.stack([v[g][:, e[g]] for g in range(8)])).reshape(128, -1)
def cut(t, i, w=512):
    return t[:, w * i:w * i + w]
def f(rng, *shape):
    return mx_ref.flush((rng.standard_normal(shape, dtype=np.float32) * np.exp2(rng.integers(-2, 3, shape[:-1] + (1,)))).astype(BF))
def wide(rng, *shape, cols=0):
    v = rng.standard_normal(shape, dtype=np.float32) * np.exp2(rng.integers(-12, 13, shape)).astype(np.float32)
    if cols: v *= np.repeat(np.exp2(rng.integers(-cols, cols + 1, shape[:-2] + (1, shape[-1] // 4))) * (rng.random(shape[:-2] + (1, shape[-1] // 4)) > 0.0625), 4, axis=-1).astype(np.float32)
    return mx_ref.flush(v.astype(BF))
K, T, O = 256, 256, 3
SH = (7, 6, 5, 4, 3, 2, 1, 0)
A = (1531, 797, 1877, 1129, 619, 1993, 1367, 911)
B = (1013, 1741, 587, 1459, 1907, 733, 1229, 1667)
def levels(q):
    return list(range(8 // N * q, 8 // N * (q + 1)))
def owned(t):
    t = t.reshape(N, 8, 16, -1).copy()
    for q in range(N):
        for g in range(8):
            if g not in levels(q): t[q, g] = 0
    return t.reshape(N, 128, -1)
def pack(p):
    return np.stack([table(p[r]) for r in range(N)])
def places(rng):
    return {"px": pack(rng.integers(0, 1024, (N, T))), "py": pack(rng.integers(0, 1024, (N, T)))}
def setup_inputs(rng):
    return {"tb": owned(f(rng, N, 128, 4 * K)), **places(rng), "w": f(rng, N, 128, 512 * O)}
def setup_inputs_same(rng):
    d = setup_inputs(rng)
    d["px"] = pack(np.repeat(rng.integers(0, 1024, (N, 1)), T, axis=1)); d["py"] = pack(np.repeat(rng.integers(0, 1024, (N, 1)), T, axis=1))
    return d
def setup_inputs_corner(rng):
    d = setup_inputs(rng); c = rng.integers(0, 4, (N, T))
    for r in range(N): c[r, rng.permutation(T)[:4]] = np.arange(4)
    d["px"] = pack((c & 1) * 1023); d["py"] = pack((c >> 1) * 1023)
    return d
def setup_inputs_alike(rng):
    d = setup_inputs(rng)
    d["px"] = pack(np.repeat(rng.integers(0, 1024, (1, T)), N, axis=0)); d["py"] = pack(np.repeat(rng.integers(0, 1024, (1, T)), N, axis=0))
    return d
def setup_inputs_line(rng):
    d = setup_inputs(rng)
    d["px"] = pack(rng.integers(0, 1025 - T, (N, 1)) + np.arange(T)); d["py"] = pack(np.repeat(rng.integers(0, 1024, (N, 1)), T, axis=1))
    return d
def setup_inputs_spread(rng):
    d = setup_inputs(rng); d["tb"] = owned(wide(rng, N, 128, 4 * K, cols=4)); return d
def check_inputs(d):
    b = []
    for r in range(N):
        for n in ("px", "py"):
            e = entries(d[n][r])
            if e.min() < 0 or e.max() > 1023: b.append(n)
        t = d["tb"][r].reshape(8, 16, -1).astype(np.float32)
        if any((t[g] != 0).any() for g in range(8) if g not in levels(r)): b.append("tb")
    return b
def addresses(x, y):
    return np.stack([((x >> SH[g]) * A[g] + (y >> SH[g]) * B[g]) & (K - 1) for g in range(8)])
def reference(tb, px, py, w):
    y = np.zeros((N, 128, O * T), np.float32)
    for r in range(N):
        e = addresses(entries(px[r]), entries(py[r])); E = []
        for q in range(N):
            a = np.full((8, T), -1); a[levels(q)] = e[levels(q)]
            E.append(mx_ref.quantize(np.ascontiguousarray(gcols(tb[q], a))))
        for o in range(O):
            W = mx_ref.quantize(np.ascontiguousarray(cut(w[r], o)))
            Z = mx_ref.matmul(W, E[0])
            for q in range(1, N): Z = Z + mx_ref.matmul(W, E[q])
            y[r][:, T * o:T * o + T] = Z
    return {"y": y}

from concourse.bass import DstId, RemoteDMATransfer
from concourse.mybir import dt, AluOpType, ActivationFunctionType

K, TOK, O, G = 256, 256, 3, 8
SH = (7, 6, 5, 4, 3, 2, 1, 0)
A = (1531, 797, 1877, 1129, 619, 1993, 1367, 911)
B = (1013, 1741, 587, 1459, 1907, 733, 1229, 1667)
SIDE = 1024
JOINT = [l for l in range(G) if (SIDE >> SH[l]) ** 2 <= K]
JSH = min(SH[l] for l in JOINT)
JROW = SIDE >> JSH
UNITS = [(tuple(JOINT), JSH, 1, JROW)] + [((l,), SH[l], A[l], B[l]) for l in range(G) if l not in JOINT]
U = len(UNITS)
C16 = TOK // 16
H = K // 2
BANKS = 8

SCRATCH = {
    "tbs": ("sbuf", [128, 4 * K], "bfloat16"), "tbg": ("sbuf", [128, 4 * K], "bfloat16"),
    "qc": ("sbuf", [128, K], "float8_e4m3fn_x4"), "qp": ("sbuf", [128, K], "uint8"),
    "wb": ("sbuf", [128, 512 * O], "bfloat16"),
    "wc": ("sbuf", [128, 128 * O], "float8_e4m3fn_x4"), "wp": ("sbuf", [128, 128 * O], "uint8"),
    "hc": ("sbuf", [128, H], "float8_e4m3fn_x4"), "hp": ("sbuf", [128, H], "uint8"),
    "lc": ("sbuf", [128, G * K], "float8_e4m3fn_x4"), "lp": ("sbuf", [128, G * K], "uint8"),
    "pxy": ("sbuf", [128, 2 * C16], "int32"), "mul": ("sbuf", [128, U * 2 * C16], "int32"),
    "s1": ("sbuf", [128, U * 2 * C16], "int32"), "s2": ("sbuf", [128, U * 2 * C16], "int32"),
    "s3": ("sbuf", [128, U * C16], "int32"), "s4": ("sbuf", [128, U * C16], "int32"),
    "lst": ("sbuf", [128, U * C16], "uint16"),
    "e0": ("sbuf", [128, 64], "int32"), "ex": ("sbuf", [128, 64], "int32"), "ey": ("sbuf", [128, 64], "int32"),
    "et": ("sbuf", [128, 64], "int32"), "ex2": ("sbuf", [128, 64], "int32"), "ey2": ("sbuf", [128, 64], "int32"),
    "es": ("sbuf", [128, 64], "int32"), "em": ("sbuf", [128, 64], "int32"), "ef": ("sbuf", [128, 64], "int32"),
    "eo": ("sbuf", [128, 64], "uint16"),
    "pick": ("sbuf", [128, U * O * K], "float32"), "acc": ("sbuf", [128, O * TOK], "float32"),
    "ps": ("psum", [128, 512 * BANKS], "float32"),
}
SEMAPHORES = ["ldt", "ldw", "ldl", "v", "c", "m", "ix", "h", "loc", "sty"] + ["t%d" % q for q in range(G)]


def bits(engines):
    return sum(1 << e for e in engines)


def direct(topo, src, ranks):
    return [d for d in ranks if d != src and topo.may_write(src, d)]


def far(topo, src, ranks):
    return [d for d in ranks if d != src and not topo.may_write(src, d)]


def far_near(topo, src, ranks):
    return [d for d in far(topo, src, ranks) if topo.die(d) == topo.die(src)]


def helpers(topo, src, ranks):
    f = far(topo, src, ranks)
    return [c for c in topo.cores_of(src) if c not in ranks and topo.die(c) == topo.die(src)
            and all(topo.may_write(c, d) for d in f)][:2]


def xfer(topo, core, dsts, engines, sem, src, outs):
    ids = []
    for d in dsts:
        rid, pid = topo.addr(d, core)
        ids.append(DstId(rid=rid, pnc=pid))
    return RemoteDMATransfer(dst_ids=ids, dma_engine_mask=bits(engines), remote_sem=sem, srcs=[src], dsts=outs, alu_op=0)


def helper_program(g, core, T, topo, ranks):
    for r, src in enumerate(ranks):
        hs = helpers(topo, src, ranks)
        if core not in hs:
            continue
        h = hs.index(core)
        dsts = far_near(topo, src, ranks)
        eng = [e for e in topo.engines(core, dsts[0]) if all(e in topo.engines(core, d) for d in dsts)]
        a, b = K * r + H * h, K * r + H * h + H
        sem = T.sem["t%d" % r]
        g.wait_ge(T.sem.h, 8)
        g.remote_dma_fused([xfer(topo, core, dsts, eng, sem, T.hc[:].bitcast(dt.uint8),
                                 [T.lc[:, a:b].bitcast(dt.uint8) for _ in dsts])], local_sem=T.sem.loc)
        g.remote_dma_fused([xfer(topo, core, dsts, eng, sem, T.hp[:], [T.lp[:, a:b] for _ in dsts])], local_sem=T.sem.loc)
        g.wait_ge(T.sem.loc, 2 * len(eng))


def rank_program(g, core, T, topo):
    ranks = list(T.cores)
    rank = T.rank_of(core)
    if rank is None:
        helper_program(g, core, T, topo, ranks)
        return
    Op, AF = AluOpType, ActivationFunctionType
    sem = T.sem
    lvl = lambda q: sem["t%d" % q]

    dirs = direct(topo, core, ranks)
    mate = [d for d in dirs if d in topo.cores_of(core)][0]
    plane = [d for d in dirs if d != mate]
    hs = helpers(topo, core, ranks)
    off = topo.engines(core, plane[0])
    every = topo.engines(core, mate)
    rest = [e for e in every if e not in off]
    fwd = [q for q, c in enumerate(ranks) if core in far_near(topo, c, ranks)]

    def kind(q):
        c = ranks[q]
        if c == core:
            return 0
        if c == mate:
            return 1
        if topo.may_write(c, core):
            return 2
        return 3 if q in fwd else 4

    def expected(q):
        k = kind(q)
        if k == 1:
            return 2 * len(rest)
        if k == 2:
            return 2 * len(off)
        if k == 3:
            return 4 * len(off)
        return 2 * len(every)

    units = sorted(UNITS, key=lambda u: max(kind(l) for l in u[0]))
    seq = [(u, o) for u in range(U) for o in range(O)]
    joint = rank in JOINT

    g.sync.dma_start(T.tbs[:], T.tb[:]).then_inc(sem.ldt, 16)
    g.sync.dma_start(T.wb[:], T.w[:]).then_inc(sem.ldw, 16)
    n = 0
    for i in range(8):
        for t, name in enumerate(("px", "py")):
            q = g.scalar if n % 4 != 3 else g.sync
            q.dma_start(T.pxy[16 * i:16 * i + 16, C16 * t:C16 * t + C16], T[name][:]).then_inc(sem.ldl, 16)
            n += 1

    cmark, nc = {}, 0
    plan = [("half",)] if joint else []
    for u in range(U):
        plan += [("cp", u, o) for o in range(O)]
        if u == 1:
            plan += [("ga", 0, O - 1)]
    for x in plan:
        nc += 1
        cmark[x] = nc

    vn = [0]

    def v(inst):
        inst.then_inc(sem.v, 1)
        vn[0] += 1
        return vn[0]

    vec = g.vector
    if joint:
        g.iota(T.e0[:], [[16, 64]], -16 * rank, 1).then_inc(sem.ix, 1)
        d = SH[rank] - JSH
        lg = JROW.bit_length() - 1
        vec.wait_ge(sem.ix, 1)
        v(vec.tensor_scalar(T.ex[:], T.e0[:], 2 + d, (JROW >> d) - 1, Op.arith_shift_right, Op.bitwise_and))
        v(vec.tensor_scalar(T.ey[:], T.e0[:], 2 + lg + d, (JROW >> d) - 1, Op.arith_shift_right, Op.bitwise_and))
        m = v(vec.tensor_scalar(T.et[:], T.e0[:], 3, None, Op.bitwise_and))
        vec.wait_ge(sem.v, m)
        v(vec.tensor_scalar(T.ex2[:], T.ex[:], 4 * A[rank], None, Op.mult))
        m = v(vec.tensor_scalar(T.ey2[:], T.ey[:], 4 * B[rank], None, Op.mult))
        vec.wait_ge(sem.v, m)
        m = v(vec.tensor_tensor(T.es[:], T.ex2[:], T.ey2[:], Op.add))
        vec.wait_ge(sem.v, m)
        m = v(vec.tensor_scalar(T.em[:], T.es[:], 4 * K - 1, None, Op.bitwise_and))
        vec.wait_ge(sem.v, m)
        m = v(vec.tensor_tensor(T.ef[:], T.em[:], T.et[:], Op.add))
        vec.wait_ge(sem.v, m)
        eo = v(vec.tensor_copy(T.eo[:], T.ef[:]))
    for u, (_, _, a, b) in enumerate(units):
        v(vec.memset(T.mul[:, 2 * C16 * u:2 * C16 * u + C16], a))
        mulm = v(vec.memset(T.mul[:, 2 * C16 * u + C16:2 * C16 * u + 2 * C16], b))
    vec.wait_ge(sem.ldt, 16)
    tile = T.tbs
    if joint:
        vec.wait_ge(sem.v, eo)
        m = v(vec.tensor_copy(T.tbg[:, 0:2 * K], T.tbs[:].indirect(T.eo[:, 0:32])))
        vec.wait_ge(sem.v, m)
        vec.wait_ge(sem.c, cmark[("half",)])
        tile = T.tbg
    qt = v(vec.quantize_mx(T.qc[:], T.qp[:], tile[:]))
    vec.wait_ge(sem.ldw, 16)
    qw = v(vec.quantize_mx(T.wc[:], T.wp[:], T.wb[:]))
    vec.wait_ge(sem.ldl, 256)
    for u, (_, sh, _, _) in enumerate(units):
        s = slice(2 * C16 * u, 2 * C16 * u + 2 * C16)
        m = v(vec.tensor_scalar(T.s1[:, s], T.pxy[:], sh, None, Op.arith_shift_right))
    vec.wait_ge(sem.v, m)
    m = v(vec.tensor_tensor(T.s2[:], T.s1[:], T.mul[:], Op.mult))
    vec.wait_ge(sem.v, m)
    for u in range(U):
        a = 2 * C16 * u
        m = v(vec.tensor_tensor(T.s3[:, C16 * u:C16 * u + C16], T.s2[:, a:a + C16], T.s2[:, a + C16:a + 2 * C16], Op.add))
    vec.wait_ge(sem.v, m)
    m = v(vec.tensor_scalar(T.s4[:], T.s3[:], K - 1, None, Op.bitwise_and))
    vec.wait_ge(sem.v, m)
    ml = v(vec.tensor_copy(T.lst[:], T.s4[:]))
    vec.wait_ge(sem.v, ml)

    def picked(u, o):
        a = K * (O * u + o)
        return T.pick[:, a:a + K].indirect(T.lst[:, C16 * u:C16 * u + C16])

    last = [0] * O
    for u, o in seq:
        out = T.acc[:, TOK * o:TOK * o + TOK]
        if u == 0:
            if ("ga", u, o) in cmark:
                continue
            vec.wait_ge(sem.c, cmark[("cp", u, o)])
            last[o] = v(vec.tensor_copy(out, picked(u, o)))
            continue
        need = cmark[("cp", u, o)]
        if u == 1 and ("ga", 0, o) in cmark:
            need = max(need, cmark[("ga", 0, o)])
        vec.wait_ge(sem.c, need)
        if last[o]:
            vec.wait_ge(sem.v, last[o])
        last[o] = v(vec.tensor_tensor(out, picked(u, o), out, Op.add))

    total = 0
    g.wait_ge(sem.v, qt)
    half = len(rest) // 2
    he = [rest[:half], rest[half:2 * half]]
    g.remote_dma_fused([xfer(topo, core, [c], he[i], sem.h, T.qc[:, H * i:H * i + H].bitcast(dt.uint8),
                             [T.hc[:].bitcast(dt.uint8)]) for i, c in enumerate(hs)], local_sem=sem.loc)
    g.remote_dma_fused([xfer(topo, core, [c], he[i], sem.h, T.qp[:, H * i:H * i + H],
                             [T.hp[:]]) for i, c in enumerate(hs)], local_sem=sem.loc)
    total += 4 * half
    s = slice(K * rank, K * rank + K)
    g.remote_dma_fused([xfer(topo, core, d, e, lvl(rank), T.qc[:].bitcast(dt.uint8), [T.lc[:, s].bitcast(dt.uint8) for _ in d])
                        for d, e in (([mate], rest), (plane, off))], local_sem=sem.loc)
    g.remote_dma_fused([xfer(topo, core, d, e, lvl(rank), T.qp[:], [T.lp[:, s] for _ in d])
                        for d, e in (([mate], rest), (plane, off))], local_sem=sem.loc)
    total += 2 * (len(rest) + len(off))
    rid, pid = topo.addr(mate, core)
    for q in fwd:
        s = slice(K * q, K * q + K)
        g.wait_ge(lvl(q), expected(q))
        g.remote_dma(T.lc[:, s].bitcast(dt.uint8), T.lc[:, s].bitcast(dt.uint8), lvl(q), sem.loc, pid, rid, bits(every))
        g.remote_dma(T.lp[:, s], T.lp[:, s], lvl(q), sem.loc, pid, rid, bits(every))
        total += 2 * len(every)
    g.wait_ge(sem.loc, total)

    pe = g.tensor
    pe.wait_ge(sem.v, qw)
    for u in range(U):
        ls = sorted(units[u][0], key=kind)
        for i, l in enumerate(ls):
            if kind(l):
                pe.wait_ge(lvl(l), expected(l))
                co, sc = T.lc[:, K * l:K * l + K], T.lp[:, K * l:K * l + K]
            else:
                co, sc = T.qc[:], T.qp[:]
            for o in range(O):
                k = O * u + o
                if i == 0 and k >= BANKS:
                    pe.wait_ge(sem.c, cmark[("cp",) + seq[k - BANKS]])
                b = 512 * (k % BANKS)
                x = pe.matmul_mx(T.ps[:, b:b + K], T.wc[:, 128 * o:128 * o + 128], T.wp[:, 128 * o:128 * o + 128],
                                 co, sc, i == 0, i == len(ls) - 1)
                if i == len(ls) - 1:
                    x.then_inc(sem.m, 1)

    act = g.scalar
    for x in plan:
        if x[0] == "half":
            act.wait_ge(sem.ldt, 16)
            act.wait_ge(sem.v, eo)
            y = act.activation(T.tbg[:, 2 * K:4 * K], T.tbs[:].indirect(T.eo[:, 32:64]), AF.Copy)
        elif x[0] == "cp":
            k = O * x[1] + x[2]
            act.wait_ge(sem.m, k + 1)
            b = 512 * (k % BANKS)
            y = act.activation(T.pick[:, K * k:K * k + K], T.ps[:, b:b + K], AF.Copy)
        else:
            u, o = x[1], x[2]
            act.wait_ge(sem.v, ml)
            act.wait_ge(sem.c, cmark[("cp", u, o)])
            y = act.activation(T.acc[:, TOK * o:TOK * o + TOK], picked(u, o), AF.Copy)
        y.then_inc(sem.c, 1)

    for o in range(O):
        g.sync.wait_ge(sem.v, last[o])
        g.sync.dma_start(T.y[:, TOK * o:TOK * o + TOK], T.acc[:, TOK * o:TOK * o + TOK]).then_inc(sem.sty, 16)
    g.sync.wait_ge(sem.sty, 16 * O)
